import numpy as np
import ml_dtypes


def mxq(x, axis, fmt="e4m3"):
    dtype, down = {"e4m3": (ml_dtypes.float8_e4m3fn, 7), "e5m2": (ml_dtypes.float8_e5m2, 14)}[fmt]
    v = np.moveaxis(np.asarray(x, np.float32).astype(ml_dtypes.bfloat16).astype(np.float64), axis, -1)
    blocks = v.reshape(v.shape[:-1] + (-1, 32))
    amax = np.abs(blocks).max(-1, keepdims=True)
    byte = np.maximum(np.where(amax > 0, np.frexp(amax)[1] - 1 + 127, 0) - down, 1)
    scale = np.exp2(byte - 127.0)
    codes = (blocks / scale).astype(np.float32).astype(dtype).astype(np.float64)
    return np.moveaxis((codes * scale).reshape(v.shape), -1, axis)


WIDE = False


def mx_kscale(k):
    if not WIDE:
        return np.ones(k)
    levels = np.array([10, -10, 5, -5, 0])
    if k % 512:
        return np.exp2(np.random.permutation(np.resize(levels, k // 32))).repeat(32)
    a = np.empty((k // 512, 16))
    for p in range(k // 512):
        a[p, :8] = np.random.permutation(np.resize(levels, 8))
        for g in range(8):
            far = levels[np.abs(levels - a[p, g]) >= 10]
            a[p, g + 8] = far[np.random.randint(len(far))]
    return np.exp2(a.ravel()).repeat(32)


def f64(x):
    return np.asarray(x).astype(np.float64)


def striped(idx):
    return np.tile(idx.reshape(-1, 16).T, (8, 1)).astype(np.uint16)


def unstriped(offs):
    return offs[:16].T.reshape(-1).astype(np.int64)


def pack_weight(w):
    k, n = w.shape
    w = f64(np.asarray(w, np.float32).astype(ml_dtypes.bfloat16)).reshape(k // 32, 32, n)
    amax = np.abs(w).max(1)
    byte = np.clip(np.where(amax > 0, np.frexp(amax)[1] - 1 + 127 - 7, 1), 1, 254)
    scaled = (w * np.exp2(127.0 - byte)[:, None, :]).reshape(k, n).astype(np.float32)
    words = np.ascontiguousarray(scaled.reshape(k // 512, 128, 4, n).transpose(0, 1, 3, 2)).astype(ml_dtypes.float8_e4m3fn).view(np.uint8)
    return words, np.ascontiguousarray(byte.astype(np.uint8).reshape(k // 512, 16, n))


def unpack_weight(words, scales):
    g, p, n, _ = words.shape
    vals = np.ascontiguousarray(words).view(ml_dtypes.float8_e4m3fn).astype(np.float64) * np.repeat(np.exp2(scales.astype(np.float64) - 127.0), 8, axis=1)[..., None]
    return vals.transpose(0, 1, 3, 2).reshape(g * 512, n)


K, T, S, N = 512, 2048, 512, 256


def setup_inputs():
    n = np.random.standard_normal
    s = mx_kscale(K)[:, None]
    words, scales = pack_weight(n((K, N)) / np.sqrt(K) / s)
    return {
        "xT": (n((K, T)) * s).astype(np.float32),
        "w_words": words,
        "w_scales": scales,
        "b": (0.3 * n((N, 1))).astype(np.float32),
        "offs": striped(np.sort(np.random.permutation(T)[:S])),
    }


def reference(xT, w_words, w_scales, b, offs):
    w = unpack_weight(w_words, w_scales)
    idx = unstriped(offs)
    xq = mxq(f64(xT)[:, idx], 0, "e4m3")
    y = w.T @ xq
    y = y + f64(b)
    return y

@@ -1,0 +1,91 @@
+from contextlib import ExitStack
+
+import concourse.mybir as mybir
+
+K, T, S, N = 512, 2048, 512, 256
+FLOPS = 2 * K * S * N
+
+F32 = mybir.dt.float32
+BF16 = mybir.dt.bfloat16
+I32 = mybir.dt.int32
+U32 = mybir.dt.uint32
+U16 = mybir.dt.uint16
+U8 = mybir.dt.uint8
+FP8X4 = mybir.dt.float8_e4m3fn_x4
+IDENTITY = mybir.ActivationFunctionType.Identity
+ADD = mybir.AluOpType.add
+
+P = 128
+PACK = 4
+HALF = S // 2
+LIST_ROWS = 16
+FIRST_WINDOW = T - S + HALF
+
+
+def tile_picked_pick_lin_bias_srt_e_kernel(tc, xT, w_words, w_scales, b, offs, out):
+    nc = tc.nc
+    with ExitStack() as ctx:
+        keep = ctx.enter_context(tc.tile_pool(name="keep", bufs=1))
+        psum = ctx.enter_context(tc.psum_pool(name="psum", bufs=1))
+
+        offsets = keep.tile([P, S // LIST_ROWS], U16, name="offsets")
+        planes = [keep.tile([P, T], F32, name="plane%d" % t, align_bytes=64) for t in range(PACK)]
+        x_rows = xT.rearrange("(p t) c -> p t c", t=PACK)
+        w_codes = keep.tile([P, N], I32, name="w_codes", align_bytes=64)
+        w_bytes = keep.tile([P, N], U8, name="w_bytes", align_bytes=64)
+        bias = keep.tile([P, N // P], F32, name="bias", align_bytes=64)
+        warm_in = keep.tile([P, 1], F32, name="warm_in", align_bytes=64)
+        warm_out = keep.tile([P, 1], F32, name="warm_out", align_bytes=64)
+
+        nc.sync.dma_start(planes[0][:], x_rows[:, 0, :])
+        nc.sync.dma_start(offsets[:], offs)
+        nc.sync.dma_start(planes[1][:], x_rows[:, 1, :])
+        nc.sync.dma_start(planes[2][:], x_rows[:, 2, :])
+        nc.sync.dma_start(planes[3][:, :FIRST_WINDOW], x_rows[:, 3, :FIRST_WINDOW])
+        nc.sync.dma_start(planes[3][:, FIRST_WINDOW:], x_rows[:, 3, FIRST_WINDOW:])
+
+        nc.vector.memset(w_bytes[:].bitcast(I32), 0)
+        nc.vector.memset(warm_in[:], 0.0)
+        nc.scalar.activation(warm_out[:], warm_in[:], IDENTITY, bias=warm_in[:])
+
+        nc.sync.dma_start(w_codes[:], w_words[0].rearrange("p n t -> p (n t)").bitcast(I32))
+        for q in range(4):
+            nc.sync.dma_start(w_bytes[32 * q : 32 * q + 4, :].bitcast(I32), w_scales[0, 4 * q : 4 * q + 4, :].bitcast(I32))
+        with nc.allow_non_contiguous_dma(reason="one bias value for each partition and output block"):
+            nc.sync.dma_start(bias[:], b.rearrange("(c p) o -> p (c o)", p=P))
+
+        picked = [keep.tile([P, HALF, PACK], BF16, name="picked%d" % h, align_bytes=64) for h in range(2)]
+        cols = HALF // LIST_ROWS
+        for t in range(PACK):
+            for h in range(2):
+                width = FIRST_WINDOW if (t == PACK - 1 and h == 0) else T
+                nc.vector.tensor_copy(picked[h][:, :, t], planes[t][:, :width].indirect(offsets[:, h * cols : (h + 1) * cols]))
+
+        x_codes = [keep.tile([P, HALF], U32, name="x_codes%d" % h, align_bytes=64) for h in range(2)]
+        x_bytes = [keep.tile([P, HALF], U8, name="x_bytes%d" % h, align_bytes=64) for h in range(2)]
+        for h in range(2):
+            nc.vector.quantize_mx(out=x_codes[h][:].bitcast(FP8X4), scales=x_bytes[h][:], in_=picked[h][:].rearrange("p n t -> p (n t)"))
+
+        for h in range(2):
+            for c in range(N // P):
+                acc = psum.tile([P, HALF], F32, name="acc%d%d" % (h, c))
+                nc.tensor.matmul_mx(
+                    out=acc[:],
+                    lhsT=w_codes[:, c * P : (c + 1) * P].bitcast(FP8X4),
+                    lhsT_scale=w_bytes[:, c * P : (c + 1) * P],
+                    rhs=x_codes[h][:].bitcast(FP8X4),
+                    rhs_scale=x_bytes[h][:],
+                    start=True,
+                    stop=True,
+                )
+                result = keep.tile([P, HALF], F32, name="result%d%d" % (h, c), align_bytes=64)
+                target = out[c * P : (c + 1) * P, h * HALF : (h + 1) * HALF]
+                if h == 1 and c == 0:
+                    nc.vector.tensor_scalar(result[:], acc[:], bias[:, c : c + 1], None, ADD)
+                    nc.sync.dma_start(target, result[:])
+                else:
+                    nc.scalar.activation(result[:], acc[:], IDENTITY, bias=bias[:, c : c + 1])
+                    if h == 0:
+                        nc.sync.dma_start(target, result[:])
+                    else:
+                        nc.scalar.dma_start(target, result[:])

@@ -1,6 +1,7 @@
 from contextlib import ExitStack
 
 import concourse.mybir as mybir
+from concourse.masks import make_identity
 
 K, T, S, N = 512, 2048, 512, 256
 FLOPS = 2 * K * S * N
@@ -13,13 +14,15 @@ U16 = mybir.dt.uint16
 U8 = mybir.dt.uint8
 FP8X4 = mybir.dt.float8_e4m3fn_x4
 IDENTITY = mybir.ActivationFunctionType.Identity
+COPY = mybir.ActivationFunctionType.Copy
 ADD = mybir.AluOpType.add
 
 P = 128
 PACK = 4
 HALF = S // 2
+QUARTER = S // 4
 LIST_ROWS = 16
-FIRST_WINDOW = T - S + HALF
+SPLIT = T - S + HALF
 
 
 def tile_picked_pick_lin_bias_srt_e_kernel(tc, xT, w_words, w_scales, b, offs, out):
@@ -30,6 +33,7 @@ def tile_picked_pick_lin_bias_srt_e_kernel(tc, xT, w_words, w_scales, b, offs, o
 
         offsets = keep.tile([P, S // LIST_ROWS], U16, name="offsets")
         planes = [keep.tile([P, T], F32, name="plane%d" % t, align_bytes=64) for t in range(PACK)]
+        rounded = [keep.tile([P, T], BF16, name="rounded%d" % t, align_bytes=64) for t in range(2)]
         x_rows = xT.rearrange("(p t) c -> p t c", t=PACK)
         w_codes = keep.tile([P, N], I32, name="w_codes", align_bytes=64)
         w_bytes = keep.tile([P, N], U8, name="w_bytes", align_bytes=64)
@@ -39,10 +43,11 @@ def tile_picked_pick_lin_bias_srt_e_kernel(tc, xT, w_words, w_scales, b, offs, o
 
         nc.sync.dma_start(planes[0][:], x_rows[:, 0, :])
         nc.sync.dma_start(offsets[:], offs)
-        nc.sync.dma_start(planes[1][:], x_rows[:, 1, :])
         nc.sync.dma_start(planes[2][:], x_rows[:, 2, :])
-        nc.sync.dma_start(planes[3][:, :FIRST_WINDOW], x_rows[:, 3, :FIRST_WINDOW])
-        nc.sync.dma_start(planes[3][:, FIRST_WINDOW:], x_rows[:, 3, FIRST_WINDOW:])
+        nc.sync.dma_start(planes[1][:, :SPLIT], x_rows[:, 1, :SPLIT])
+        nc.sync.dma_start(planes[3][:, :SPLIT], x_rows[:, 3, :SPLIT])
+        nc.sync.dma_start(planes[1][:, SPLIT:], x_rows[:, 1, SPLIT:])
+        nc.sync.dma_start(planes[3][:, SPLIT:], x_rows[:, 3, SPLIT:])
 
         nc.vector.memset(w_bytes[:].bitcast(I32), 0)
         nc.vector.memset(warm_in[:], 0.0)
@@ -56,36 +61,51 @@ def tile_picked_pick_lin_bias_srt_e_kernel(tc, xT, w_words, w_scales, b, offs, o
 
         picked = [keep.tile([P, HALF, PACK], BF16, name="picked%d" % h, align_bytes=64) for h in range(2)]
         cols = HALF // LIST_ROWS
-        for t in range(PACK):
-            for h in range(2):
-                width = FIRST_WINDOW if (t == PACK - 1 and h == 0) else T
-                nc.vector.tensor_copy(picked[h][:, :, t], planes[t][:, :width].indirect(offsets[:, h * cols : (h + 1) * cols]))
+        lists = [offsets[:, h * cols : (h + 1) * cols] for h in range(2)]
 
-        x_codes = [keep.tile([P, HALF], U32, name="x_codes%d" % h, align_bytes=64) for h in range(2)]
-        x_bytes = [keep.tile([P, HALF], U8, name="x_bytes%d" % h, align_bytes=64) for h in range(2)]
-        for h in range(2):
-            nc.vector.quantize_mx(out=x_codes[h][:].bitcast(FP8X4), scales=x_bytes[h][:], in_=picked[h][:].rearrange("p n t -> p (n t)"))
+        nc.vector.tensor_copy(picked[0][:, :, 0], planes[0][:].indirect(lists[0]))
+        nc.scalar.activation(rounded[0][:], planes[0][:], COPY)
+        nc.scalar.activation(picked[1][:, :, 0], rounded[0][:].indirect(lists[1]), COPY)
+        nc.vector.tensor_copy(picked[0][:, :, 2], planes[2][:].indirect(lists[0]))
+        nc.vector.tensor_copy(picked[1][:, :, 2], planes[2][:].indirect(lists[1]))
+        nc.vector.tensor_copy(picked[0][:, :, 1], planes[1][:, :SPLIT].indirect(lists[0]))
+        nc.scalar.activation(rounded[1][:, :SPLIT], planes[1][:, :SPLIT], COPY)
+        nc.vector.tensor_copy(picked[0][:, :, 3], planes[3][:, :SPLIT].indirect(lists[0]))
+        nc.scalar.activation(rounded[1][:, SPLIT:], planes[1][:, SPLIT:], COPY)
+        nc.scalar.activation(picked[1][:, :, 1], rounded[1][:].indirect(lists[1]), COPY)
+        nc.vector.tensor_copy(picked[1][:, :, 3], planes[3][:].indirect(lists[1]))
 
-        for h in range(2):
+        acc = [[psum.tile([P, 4 * P], F32, name="acc%d%d" % (q, c)) for c in range(N // P)] for q in range(4)]
+        identity = keep.tile([P, P], F32, name="identity", align_bytes=64)
+        make_identity(nc, identity[:])
+        spare = acc[3][1]
+        for source, count in ((planes[1][:, :P], 13), (planes[3][:, :P], 8), (planes[3][:, SPLIT : SPLIT + P], 6)):
+            for i in range(count):
+                nc.tensor.transpose(spare[:, (i % 4) * P : (i % 4 + 1) * P], source, identity[:])
+
+        x_codes = [keep.tile([P, QUARTER], U32, name="x_codes%d" % q, align_bytes=64) for q in range(4)]
+        x_bytes = [keep.tile([P, QUARTER], U8, name="x_bytes%d" % q, align_bytes=64) for q in range(4)]
+        for q in range(4):
+            h, u = divmod(q, 2)
+            nc.vector.quantize_mx(out=x_codes[q][:].bitcast(FP8X4), scales=x_bytes[q][:], in_=picked[h][:, u * QUARTER : (u + 1) * QUARTER, :].rearrange("p n t -> p (n t)"))
+
+        result = [[keep.tile([P, HALF], F32, name="result%d%d" % (h, c), align_bytes=64) for c in range(N // P)] for h in range(2)]
+        for q in range(4):
+            h, u = divmod(q, 2)
             for c in range(N // P):
-                acc = psum.tile([P, HALF], F32, name="acc%d%d" % (h, c))
                 nc.tensor.matmul_mx(
-                    out=acc[:],
+                    out=acc[q][c][:, :QUARTER],
                     lhsT=w_codes[:, c * P : (c + 1) * P].bitcast(FP8X4),
                     lhsT_scale=w_bytes[:, c * P : (c + 1) * P],
-                    rhs=x_codes[h][:].bitcast(FP8X4),
-                    rhs_scale=x_bytes[h][:],
+                    rhs=x_codes[q][:].bitcast(FP8X4),
+                    rhs_scale=x_bytes[q][:],
                     start=True,
                     stop=True,
                 )
-                result = keep.tile([P, HALF], F32, name="result%d%d" % (h, c), align_bytes=64)
-                target = out[c * P : (c + 1) * P, h * HALF : (h + 1) * HALF]
-                if h == 1 and c == 0:
-                    nc.vector.tensor_scalar(result[:], acc[:], bias[:, c : c + 1], None, ADD)
-                    nc.sync.dma_start(target, result[:])
+                piece = result[h][c][:, u * QUARTER : (u + 1) * QUARTER]
+                if c == 0:
+                    nc.scalar.activation(piece, acc[q][c][:, :QUARTER], IDENTITY, bias=bias[:, c : c + 1])
                 else:
-                    nc.scalar.activation(result[:], acc[:], IDENTITY, bias=bias[:, c : c + 1])
-                    if h == 0:
-                        nc.sync.dma_start(target, result[:])
-                    else:
-                        nc.scalar.dma_start(target, result[:])
+                    nc.vector.tensor_scalar(piece, acc[q][c][:, :QUARTER], bias[:, c : c + 1], None, ADD)
+                if u == 1:
+                    nc.sync.dma_start(out[c * P : (c + 1) * P, h * HALF : (h + 1) * HALF], result[h][c][:])

@@ -23,6 +23,7 @@ HALF = S // 2
 QUARTER = S // 4
 LIST_ROWS = 16
 SPLIT = T - S + HALF
+CAST_SPLIT = 1024
 
 
 def tile_picked_pick_lin_bias_srt_e_kernel(tc, xT, w_words, w_scales, b, offs, out):
@@ -32,7 +33,8 @@ def tile_picked_pick_lin_bias_srt_e_kernel(tc, xT, w_words, w_scales, b, offs, o
         psum = ctx.enter_context(tc.psum_pool(name="psum", bufs=1))
 
         offsets = keep.tile([P, S // LIST_ROWS], U16, name="offsets")
-        planes = [keep.tile([P, T], F32, name="plane%d" % t, align_bytes=64) for t in range(PACK)]
+        low = keep.tile([P, 2 * T], F32, name="low", align_bytes=64)
+        planes = [low[:, :T], low[:, T:]] + [keep.tile([P, T], F32, name="plane%d" % t, align_bytes=64)[:] for t in (2, 3)]
         rounded = [keep.tile([P, T], BF16, name="rounded%d" % t, align_bytes=64) for t in range(2)]
         x_rows = xT.rearrange("(p t) c -> p t c", t=PACK)
         w_codes = keep.tile([P, N], I32, name="w_codes", align_bytes=64)
@@ -41,10 +43,9 @@ def tile_picked_pick_lin_bias_srt_e_kernel(tc, xT, w_words, w_scales, b, offs, o
         warm_in = keep.tile([P, 1], F32, name="warm_in", align_bytes=64)
         warm_out = keep.tile([P, 1], F32, name="warm_out", align_bytes=64)
 
-        nc.sync.dma_start(planes[0][:], x_rows[:, 0, :])
+        nc.sync.dma_start(low[:, : T + SPLIT], x_rows.rearrange("p t c -> p (t c)")[:, : T + SPLIT])
         nc.sync.dma_start(offsets[:], offs)
         nc.sync.dma_start(planes[2][:], x_rows[:, 2, :])
-        nc.sync.dma_start(planes[1][:, :SPLIT], x_rows[:, 1, :SPLIT])
         nc.sync.dma_start(planes[3][:, :SPLIT], x_rows[:, 3, :SPLIT])
         nc.sync.dma_start(planes[1][:, SPLIT:], x_rows[:, 1, SPLIT:])
         nc.sync.dma_start(planes[3][:, SPLIT:], x_rows[:, 3, SPLIT:])
@@ -63,49 +64,57 @@ def tile_picked_pick_lin_bias_srt_e_kernel(tc, xT, w_words, w_scales, b, offs, o
         cols = HALF // LIST_ROWS
         lists = [offsets[:, h * cols : (h + 1) * cols] for h in range(2)]
 
-        nc.vector.tensor_copy(picked[0][:, :, 0], planes[0][:].indirect(lists[0]))
-        nc.scalar.activation(rounded[0][:], planes[0][:], COPY)
-        nc.scalar.activation(picked[1][:, :, 0], rounded[0][:].indirect(lists[1]), COPY)
-        nc.vector.tensor_copy(picked[0][:, :, 2], planes[2][:].indirect(lists[0]))
-        nc.vector.tensor_copy(picked[1][:, :, 2], planes[2][:].indirect(lists[1]))
+        nc.vector.tensor_copy(picked[0][:, :, 0], planes[0].indirect(lists[0]))
         nc.vector.tensor_copy(picked[0][:, :, 1], planes[1][:, :SPLIT].indirect(lists[0]))
-        nc.scalar.activation(rounded[1][:, :SPLIT], planes[1][:, :SPLIT], COPY)
+        nc.vector.tensor_copy(rounded[1][:, :CAST_SPLIT], planes[1][:, :CAST_SPLIT])
+        nc.scalar.activation(rounded[0][:], planes[0], COPY)
+        nc.scalar.activation(rounded[1][:, CAST_SPLIT:SPLIT], planes[1][:, CAST_SPLIT:SPLIT], COPY)
+        nc.scalar.activation(picked[1][:, :, 0], rounded[0][:].indirect(lists[1]), COPY)
+        nc.vector.tensor_copy(picked[0][:, :, 2], planes[2].indirect(lists[0]))
+        nc.vector.tensor_copy(picked[1][:, :, 2], planes[2].indirect(lists[1]))
         nc.vector.tensor_copy(picked[0][:, :, 3], planes[3][:, :SPLIT].indirect(lists[0]))
         nc.scalar.activation(rounded[1][:, SPLIT:], planes[1][:, SPLIT:], COPY)
         nc.scalar.activation(picked[1][:, :, 1], rounded[1][:].indirect(lists[1]), COPY)
-        nc.vector.tensor_copy(picked[1][:, :, 3], planes[3][:].indirect(lists[1]))
+        nc.vector.tensor_copy(picked[1][:, :, 3], planes[3].indirect(lists[1]))
 
         acc = [[psum.tile([P, 4 * P], F32, name="acc%d%d" % (q, c)) for c in range(N // P)] for q in range(4)]
         identity = keep.tile([P, P], F32, name="identity", align_bytes=64)
         make_identity(nc, identity[:])
+        held = keep.tile([P, HALF], F32, name="held", tag="held", align_bytes=64)
+        make_identity(nc, held[:, :P])
         spare = acc[3][1]
-        for source, count in ((planes[1][:, :P], 13), (planes[3][:, :P], 8), (planes[3][:, SPLIT : SPLIT + P], 6)):
+        for source, count in ((planes[2][:, :P], 13), (planes[3][:, :P], 6)):
             for i in range(count):
                 nc.tensor.transpose(spare[:, (i % 4) * P : (i % 4 + 1) * P], source, identity[:])
+        for i in range(6):
+            nc.tensor.transpose(spare[:, (i % 4) * P : (i % 4 + 1) * P], planes[3][:, SPLIT : SPLIT + P], held[:, :P] if i == 0 else identity[:])
 
-        x_codes = [keep.tile([P, QUARTER], U32, name="x_codes%d" % q, align_bytes=64) for q in range(4)]
+        first_codes = keep.tile([P, HALF], U32, name="first_codes", tag="held", align_bytes=64)
+        second_codes = keep.tile([P, HALF], U32, name="second_codes", align_bytes=64)
+        x_codes = [codes[:, u * QUARTER : (u + 1) * QUARTER] for codes in (first_codes, second_codes) for u in range(2)]
         x_bytes = [keep.tile([P, QUARTER], U8, name="x_bytes%d" % q, align_bytes=64) for q in range(4)]
         for q in range(4):
             h, u = divmod(q, 2)
             nc.vector.quantize_mx(out=x_codes[q][:].bitcast(FP8X4), scales=x_bytes[q][:], in_=picked[h][:, u * QUARTER : (u + 1) * QUARTER, :].rearrange("p n t -> p (n t)"))
 
-        result = [[keep.tile([P, HALF], F32, name="result%d%d" % (h, c), align_bytes=64) for c in range(N // P)] for h in range(2)]
-        for q in range(4):
-            h, u = divmod(q, 2)
-            for c in range(N // P):
-                nc.tensor.matmul_mx(
-                    out=acc[q][c][:, :QUARTER],
-                    lhsT=w_codes[:, c * P : (c + 1) * P].bitcast(FP8X4),
-                    lhsT_scale=w_bytes[:, c * P : (c + 1) * P],
-                    rhs=x_codes[q][:].bitcast(FP8X4),
-                    rhs_scale=x_bytes[q][:],
-                    start=True,
-                    stop=True,
-                )
-                piece = result[h][c][:, u * QUARTER : (u + 1) * QUARTER]
-                if c == 0:
-                    nc.scalar.activation(piece, acc[q][c][:, :QUARTER], IDENTITY, bias=bias[:, c : c + 1])
-                else:
-                    nc.vector.tensor_scalar(piece, acc[q][c][:, :QUARTER], bias[:, c : c + 1], None, ADD)
-                if u == 1:
-                    nc.sync.dma_start(out[c * P : (c + 1) * P, h * HALF : (h + 1) * HALF], result[h][c][:])
+        stores = ((0, 1), (1, 2), (2, 4))
+        out_blocks = out.rearrange("(c p) j -> p c j", p=P)
+        for first, last in stores:
+            result = keep.tile([P, N // P, (last - first) * QUARTER], F32, name="result%d" % first, align_bytes=64)
+            for q in range(first, last):
+                for c in range(N // P):
+                    nc.tensor.matmul_mx(
+                        out=acc[q][c][:, :QUARTER],
+                        lhsT=w_codes[:, c * P : (c + 1) * P].bitcast(FP8X4),
+                        lhsT_scale=w_bytes[:, c * P : (c + 1) * P],
+                        rhs=x_codes[q][:].bitcast(FP8X4),
+                        rhs_scale=x_bytes[q][:],
+                        start=True,
+                        stop=True,
+                    )
+                    piece = result[:, c, (q - first) * QUARTER : (q - first + 1) * QUARTER]
+                    if c == 0:
+                        nc.scalar.activation(piece, acc[q][c][:, :QUARTER], IDENTITY, bias=bias[:, c : c + 1])
+                    else:
+                        nc.vector.tensor_scalar(piece, acc[q][c][:, :QUARTER], bias[:, c : c + 1], None, ADD)
+            nc.sync.dma_start(out_blocks[:, :, first * QUARTER : last * QUARTER], result[:])

@@ -77,17 +77,10 @@ def tile_picked_pick_lin_bias_srt_e_kernel(tc, xT, w_words, w_scales, b, offs, o
         nc.scalar.activation(picked[1][:, :, 1], rounded[1][:].indirect(lists[1]), COPY)
         nc.vector.tensor_copy(picked[1][:, :, 3], planes[3].indirect(lists[1]))
 
-        acc = [[psum.tile([P, 4 * P], F32, name="acc%d%d" % (q, c)) for c in range(N // P)] for q in range(4)]
-        identity = keep.tile([P, P], F32, name="identity", align_bytes=64)
-        make_identity(nc, identity[:])
+        acc = [[psum.tile([P, QUARTER], F32, name="acc%d%d" % (q, c)) for c in range(N // P)] for q in range(4)]
         held = keep.tile([P, HALF], F32, name="held", tag="held", align_bytes=64)
         make_identity(nc, held[:, :P])
-        spare = acc[3][1]
-        for source, count in ((planes[2][:, :P], 13), (planes[3][:, :P], 6)):
-            for i in range(count):
-                nc.tensor.transpose(spare[:, (i % 4) * P : (i % 4 + 1) * P], source, identity[:])
-        for i in range(6):
-            nc.tensor.transpose(spare[:, (i % 4) * P : (i % 4 + 1) * P], planes[3][:, SPLIT : SPLIT + P], held[:, :P] if i == 0 else identity[:])
+        nc.tensor.transpose(acc[3][1][:], planes[3][:, SPLIT : SPLIT + P], held[:, :P])
 
         first_codes = keep.tile([P, HALF], U32, name="first_codes", tag="held", align_bytes=64)
         second_codes = keep.tile([P, HALF], U32, name="second_codes", align_bytes=64)
@@ -97,7 +90,7 @@ def tile_picked_pick_lin_bias_srt_e_kernel(tc, xT, w_words, w_scales, b, offs, o
             h, u = divmod(q, 2)
             nc.vector.quantize_mx(out=x_codes[q][:].bitcast(FP8X4), scales=x_bytes[q][:], in_=picked[h][:, u * QUARTER : (u + 1) * QUARTER, :].rearrange("p n t -> p (n t)"))
 
-        stores = ((0, 1), (1, 2), (2, 4))
+        stores = ((0, 1), (1, 2), (2, 3), (3, 4))
         out_blocks = out.rearrange("(c p) j -> p c j", p=P)
         for first, last in stores:
             result = keep.tile([P, N // P, (last - first) * QUARTER], F32, name="result%d" % first, align_bytes=64)

@@ -90,14 +90,13 @@ def tile_picked_pick_lin_bias_srt_e_kernel(tc, xT, w_words, w_scales, b, offs, o
             h, u = divmod(q, 2)
             nc.vector.quantize_mx(out=x_codes[q][:].bitcast(FP8X4), scales=x_bytes[q][:], in_=picked[h][:, u * QUARTER : (u + 1) * QUARTER, :].rearrange("p n t -> p (n t)"))
 
-        stores = ((0, 1), (1, 2), (2, 3), (3, 4))
-        out_blocks = out.rearrange("(c p) j -> p c j", p=P)
-        for first, last in stores:
-            result = keep.tile([P, N // P, (last - first) * QUARTER], F32, name="result%d" % first, align_bytes=64)
-            for q in range(first, last):
-                for c in range(N // P):
+        for h in range(2):
+            for c in range(N // P):
+                result = keep.tile([P, HALF], F32, name="result%d%d" % (h, c), align_bytes=64)
+                for u in range(2):
+                    q = 2 * h + u
                     nc.tensor.matmul_mx(
-                        out=acc[q][c][:, :QUARTER],
+                        out=acc[q][c][:],
                         lhsT=w_codes[:, c * P : (c + 1) * P].bitcast(FP8X4),
                         lhsT_scale=w_bytes[:, c * P : (c + 1) * P],
                         rhs=x_codes[q][:].bitcast(FP8X4),
@@ -105,9 +104,9 @@ def tile_picked_pick_lin_bias_srt_e_kernel(tc, xT, w_words, w_scales, b, offs, o
                         start=True,
                         stop=True,
                     )
-                    piece = result[:, c, (q - first) * QUARTER : (q - first + 1) * QUARTER]
-                    if c == 0:
-                        nc.scalar.activation(piece, acc[q][c][:, :QUARTER], IDENTITY, bias=bias[:, c : c + 1])
+                    piece = result[:, u * QUARTER : (u + 1) * QUARTER]
+                    if u == 0:
+                        nc.scalar.activation(piece, acc[q][c][:], IDENTITY, bias=bias[:, c : c + 1])
                     else:
-                        nc.vector.tensor_scalar(piece, acc[q][c][:, :QUARTER], bias[:, c : c + 1], None, ADD)
-            nc.sync.dma_start(out_blocks[:, :, first * QUARTER : last * QUARTER], result[:])
+                        nc.vector.tensor_scalar(piece, acc[q][c][:], bias[:, c : c + 1], None, ADD)
+                nc.sync.dma_start(out[c * P : (c + 1) * P, h * HALF : (h + 1) * HALF], result[:])

@@ -39,26 +39,31 @@ def tile_picked_pick_lin_bias_srt_e_kernel(tc, xT, w_words, w_scales, b, offs, o
         x_rows = xT.rearrange("(p t) c -> p t c", t=PACK)
         w_codes = keep.tile([P, N], I32, name="w_codes", align_bytes=64)
         w_bytes = keep.tile([P, N], U8, name="w_bytes", align_bytes=64)
+        bias_rows = keep.tile([P, P], F32, name="bias_rows", align_bytes=64)
         bias = keep.tile([P, N // P], F32, name="bias", align_bytes=64)
         warm_in = keep.tile([P, 1], F32, name="warm_in", align_bytes=64)
         warm_out = keep.tile([P, 1], F32, name="warm_out", align_bytes=64)
 
+        def load_scales(q):
+            nc.sync.dma_start(w_bytes[32 * q : 32 * q + 4, :].bitcast(I32), w_scales[0, 4 * q : 4 * q + 4, :].bitcast(I32))
+
+        nc.vector.memset(w_bytes[:].bitcast(I32), 0)
         nc.sync.dma_start(low[:, : T + SPLIT], x_rows.rearrange("p t c -> p (t c)")[:, : T + SPLIT])
         nc.sync.dma_start(offsets[:], offs)
+        load_scales(0)
         nc.sync.dma_start(planes[2][:], x_rows[:, 2, :])
         nc.sync.dma_start(planes[3][:, :SPLIT], x_rows[:, 3, :SPLIT])
         nc.sync.dma_start(planes[1][:, SPLIT:], x_rows[:, 1, SPLIT:])
         nc.sync.dma_start(planes[3][:, SPLIT:], x_rows[:, 3, SPLIT:])
 
-        nc.vector.memset(w_bytes[:].bitcast(I32), 0)
+        nc.vector.memset(bias_rows[:], 0.0)
         nc.vector.memset(warm_in[:], 0.0)
         nc.scalar.activation(warm_out[:], warm_in[:], IDENTITY, bias=warm_in[:])
 
+        nc.sync.dma_start(bias_rows[: N // P, :], b.rearrange("(c p) o -> c (p o)", p=P))
         nc.sync.dma_start(w_codes[:], w_words[0].rearrange("p n t -> p (n t)").bitcast(I32))
-        for q in range(4):
-            nc.sync.dma_start(w_bytes[32 * q : 32 * q + 4, :].bitcast(I32), w_scales[0, 4 * q : 4 * q + 4, :].bitcast(I32))
-        with nc.allow_non_contiguous_dma(reason="one bias value for each partition and output block"):
-            nc.sync.dma_start(bias[:], b.rearrange("(c p) o -> p (c o)", p=P))
+        for q in range(1, 4):
+            load_scales(q)
 
         picked = [keep.tile([P, HALF, PACK], BF16, name="picked%d" % h, align_bytes=64) for h in range(2)]
         cols = HALF // LIST_ROWS
@@ -78,13 +83,13 @@ def tile_picked_pick_lin_bias_srt_e_kernel(tc, xT, w_words, w_scales, b, offs, o
         nc.vector.tensor_copy(picked[1][:, :, 3], planes[3].indirect(lists[1]))
 
         acc = [[psum.tile([P, QUARTER], F32, name="acc%d%d" % (q, c)) for c in range(N // P)] for q in range(4)]
-        held = keep.tile([P, HALF], F32, name="held", tag="held", align_bytes=64)
+        held = keep.tile([P, P], F32, name="held", tag="held", align_bytes=64)
         make_identity(nc, held[:, :P])
-        nc.tensor.transpose(acc[3][1][:], planes[3][:, SPLIT : SPLIT + P], held[:, :P])
+        nc.tensor.transpose(acc[3][1][:], bias_rows[:], held[:, :P])
+        nc.scalar.activation(bias[:], acc[3][1][:, : N // P], COPY)
 
-        first_codes = keep.tile([P, HALF], U32, name="first_codes", tag="held", align_bytes=64)
-        second_codes = keep.tile([P, HALF], U32, name="second_codes", align_bytes=64)
-        x_codes = [codes[:, u * QUARTER : (u + 1) * QUARTER] for codes in (first_codes, second_codes) for u in range(2)]
+        codes = keep.tile([P, S], U32, name="codes", tag="held", align_bytes=64)
+        x_codes = [codes[:, q * QUARTER : (q + 1) * QUARTER] for q in range(4)]
         x_bytes = [keep.tile([P, QUARTER], U8, name="x_bytes%d" % q, align_bytes=64) for q in range(4)]
         for q in range(4):
             h, u = divmod(q, 2)

@@ -33,16 +33,14 @@ def tile_picked_pick_lin_bias_srt_e_kernel(tc, xT, w_words, w_scales, b, offs, o
         psum = ctx.enter_context(tc.psum_pool(name="psum", bufs=1))
 
         offsets = keep.tile([P, S // LIST_ROWS], U16, name="offsets")
-        low = keep.tile([P, 2 * T], F32, name="low", align_bytes=64)
-        planes = [low[:, :T], low[:, T:]] + [keep.tile([P, T], F32, name="plane%d" % t, align_bytes=64)[:] for t in (2, 3)]
+        low = keep.tile([P, 2 * T], F32, name="low", align_bytes=512)
+        planes = [low[:, :T], low[:, T:]] + [keep.tile([P, T], F32, name="plane%d" % t, align_bytes=512)[:] for t in (2, 3)]
         rounded = [keep.tile([P, T], BF16, name="rounded%d" % t, align_bytes=64) for t in range(2)]
         x_rows = xT.rearrange("(p t) c -> p t c", t=PACK)
-        w_codes = keep.tile([P, N], I32, name="w_codes", align_bytes=64)
+        w_codes = keep.tile([P, N], I32, name="w_codes", align_bytes=512)
         w_bytes = keep.tile([P, N], U8, name="w_bytes", align_bytes=64)
         bias_rows = keep.tile([P, P], F32, name="bias_rows", align_bytes=64)
         bias = keep.tile([P, N // P], F32, name="bias", align_bytes=64)
-        warm_in = keep.tile([P, 1], F32, name="warm_in", align_bytes=64)
-        warm_out = keep.tile([P, 1], F32, name="warm_out", align_bytes=64)
 
         def load_scales(q):
             nc.sync.dma_start(w_bytes[32 * q : 32 * q + 4, :].bitcast(I32), w_scales[0, 4 * q : 4 * q + 4, :].bitcast(I32))
@@ -57,8 +55,6 @@ def tile_picked_pick_lin_bias_srt_e_kernel(tc, xT, w_words, w_scales, b, offs, o
         nc.sync.dma_start(planes[3][:, SPLIT:], x_rows[:, 3, SPLIT:])
 
         nc.vector.memset(bias_rows[:], 0.0)
-        nc.vector.memset(warm_in[:], 0.0)
-        nc.scalar.activation(warm_out[:], warm_in[:], IDENTITY, bias=warm_in[:])
 
         nc.sync.dma_start(bias_rows[: N // P, :], b.rearrange("(c p) o -> c (p o)", p=P))
         nc.sync.dma_start(w_codes[:], w_words[0].rearrange("p n t -> p (n t)").bitcast(I32))
@@ -97,7 +93,7 @@ def tile_picked_pick_lin_bias_srt_e_kernel(tc, xT, w_words, w_scales, b, offs, o
 
         for h in range(2):
             for c in range(N // P):
-                result = keep.tile([P, HALF], F32, name="result%d%d" % (h, c), align_bytes=64)
+                result = keep.tile([P, HALF], F32, name="result%d%d" % (h, c), align_bytes=512)
                 for u in range(2):
                     q = 2 * h + u
                     nc.tensor.matmul_mx(

@@ -106,7 +106,7 @@ def tile_picked_pick_lin_bias_srt_e_kernel(tc, xT, w_words, w_scales, b, offs, o
                         stop=True,
                     )
                     piece = result[:, u * QUARTER : (u + 1) * QUARTER]
-                    if u == 0:
+                    if c == 1:
                         nc.scalar.activation(piece, acc[q][c][:], IDENTITY, bias=bias[:, c : c + 1])
                     else:
                         nc.vector.tensor_scalar(piece, acc[q][c][:], bias[:, c : c + 1], None, ADD)

@@ -23,7 +23,6 @@ HALF = S // 2
 QUARTER = S // 4
 LIST_ROWS = 16
 SPLIT = T - S + HALF
-CAST_SPLIT = 1024
 
 
 def tile_picked_pick_lin_bias_srt_e_kernel(tc, xT, w_words, w_scales, b, offs, out):
@@ -35,7 +34,6 @@ def tile_picked_pick_lin_bias_srt_e_kernel(tc, xT, w_words, w_scales, b, offs, o
         offsets = keep.tile([P, S // LIST_ROWS], U16, name="offsets")
         low = keep.tile([P, 2 * T], F32, name="low", align_bytes=512)
         planes = [low[:, :T], low[:, T:]] + [keep.tile([P, T], F32, name="plane%d" % t, align_bytes=512)[:] for t in (2, 3)]
-        rounded = [keep.tile([P, T], BF16, name="rounded%d" % t, align_bytes=64) for t in range(2)]
         x_rows = xT.rearrange("(p t) c -> p t c", t=PACK)
         w_codes = keep.tile([P, N], I32, name="w_codes", align_bytes=512)
         w_bytes = keep.tile([P, N], U8, name="w_bytes", align_bytes=64)
@@ -46,12 +44,11 @@ def tile_picked_pick_lin_bias_srt_e_kernel(tc, xT, w_words, w_scales, b, offs, o
             nc.sync.dma_start(w_bytes[32 * q : 32 * q + 4, :].bitcast(I32), w_scales[0, 4 * q : 4 * q + 4, :].bitcast(I32))
 
         nc.vector.memset(w_bytes[:].bitcast(I32), 0)
-        nc.sync.dma_start(low[:, : T + SPLIT], x_rows.rearrange("p t c -> p (t c)")[:, : T + SPLIT])
+        nc.sync.dma_start(low[:], x_rows.rearrange("p t c -> p (t c)")[:, : 2 * T])
         nc.sync.dma_start(offsets[:], offs)
         load_scales(0)
         nc.sync.dma_start(planes[2][:], x_rows[:, 2, :])
         nc.sync.dma_start(planes[3][:, :SPLIT], x_rows[:, 3, :SPLIT])
-        nc.sync.dma_start(planes[1][:, SPLIT:], x_rows[:, 1, SPLIT:])
         nc.sync.dma_start(planes[3][:, SPLIT:], x_rows[:, 3, SPLIT:])
 
         nc.vector.memset(bias_rows[:], 0.0)
@@ -61,22 +58,20 @@ def tile_picked_pick_lin_bias_srt_e_kernel(tc, xT, w_words, w_scales, b, offs, o
         for q in range(1, 4):
             load_scales(q)
 
-        picked = [keep.tile([P, HALF, PACK], BF16, name="picked%d" % h, align_bytes=64) for h in range(2)]
+        pairs = [keep.tile([P, 2, HALF, 2], BF16, name="pairs%d" % h, align_bytes=64) for h in range(2)]
         cols = HALF // LIST_ROWS
         lists = [offsets[:, h * cols : (h + 1) * cols] for h in range(2)]
 
-        nc.vector.tensor_copy(picked[0][:, :, 0], planes[0].indirect(lists[0]))
-        nc.vector.tensor_copy(picked[0][:, :, 1], planes[1][:, :SPLIT].indirect(lists[0]))
-        nc.vector.tensor_copy(rounded[1][:, :CAST_SPLIT], planes[1][:, :CAST_SPLIT])
-        nc.scalar.activation(rounded[0][:], planes[0], COPY)
-        nc.scalar.activation(rounded[1][:, CAST_SPLIT:SPLIT], planes[1][:, CAST_SPLIT:SPLIT], COPY)
-        nc.scalar.activation(picked[1][:, :, 0], rounded[0][:].indirect(lists[1]), COPY)
-        nc.vector.tensor_copy(picked[0][:, :, 2], planes[2].indirect(lists[0]))
-        nc.vector.tensor_copy(picked[1][:, :, 2], planes[2].indirect(lists[1]))
-        nc.vector.tensor_copy(picked[0][:, :, 3], planes[3][:, :SPLIT].indirect(lists[0]))
-        nc.scalar.activation(rounded[1][:, SPLIT:], planes[1][:, SPLIT:], COPY)
-        nc.scalar.activation(picked[1][:, :, 1], rounded[1][:].indirect(lists[1]), COPY)
-        nc.vector.tensor_copy(picked[1][:, :, 3], planes[3].indirect(lists[1]))
+        for t in range(PACK):
+            for h in range(2):
+                window = planes[t][:, :SPLIT] if (t, h) == (PACK - 1, 0) else planes[t]
+                nc.vector.tensor_copy(pairs[h][:, t // 2, :, t % 2], window.indirect(lists[h]))
+
+        picked = [keep.tile([P, QUARTER * PACK], BF16, name="picked%d" % q, align_bytes=64) for q in range(4)]
+        for q in range(4):
+            h, u = divmod(q, 2)
+            words = pairs[h][:].rearrange("p a n e -> p (a n e)").bitcast(U32).rearrange("p (a n) -> p n a", a=2)
+            nc.scalar.copy(picked[q][:].bitcast(U32).rearrange("p (n a) -> p n a", a=2), words[:, u * QUARTER : (u + 1) * QUARTER, :])
 
         acc = [[psum.tile([P, QUARTER], F32, name="acc%d%d" % (q, c)) for c in range(N // P)] for q in range(4)]
         held = keep.tile([P, P], F32, name="held", tag="held", align_bytes=64)
@@ -88,8 +83,7 @@ def tile_picked_pick_lin_bias_srt_e_kernel(tc, xT, w_words, w_scales, b, offs, o
         x_codes = [codes[:, q * QUARTER : (q + 1) * QUARTER] for q in range(4)]
         x_bytes = [keep.tile([P, QUARTER], U8, name="x_bytes%d" % q, align_bytes=64) for q in range(4)]
         for q in range(4):
-            h, u = divmod(q, 2)
-            nc.vector.quantize_mx(out=x_codes[q][:].bitcast(FP8X4), scales=x_bytes[q][:], in_=picked[h][:, u * QUARTER : (u + 1) * QUARTER, :].rearrange("p n t -> p (n t)"))
+            nc.vector.quantize_mx(out=x_codes[q][:].bitcast(FP8X4), scales=x_bytes[q][:], in_=picked[q][:])
 
         for h in range(2):
             for c in range(N // P):

@@ -46,7 +46,8 @@ def tile_picked_pick_lin_bias_srt_e_kernel(tc, xT, w_words, w_scales, b, offs, o
         nc.vector.memset(w_bytes[:].bitcast(I32), 0)
         nc.sync.dma_start(low[:], x_rows.rearrange("p t c -> p (t c)")[:, : 2 * T])
         nc.sync.dma_start(offsets[:], offs)
-        load_scales(0)
+        for q in range(4):
+            load_scales(q)
         nc.sync.dma_start(planes[2][:], x_rows[:, 2, :])
         nc.sync.dma_start(planes[3][:, :SPLIT], x_rows[:, 3, :SPLIT])
         nc.sync.dma_start(planes[3][:, SPLIT:], x_rows[:, 3, SPLIT:])
@@ -55,10 +56,8 @@ def tile_picked_pick_lin_bias_srt_e_kernel(tc, xT, w_words, w_scales, b, offs, o
 
         nc.sync.dma_start(bias_rows[: N // P, :], b.rearrange("(c p) o -> c (p o)", p=P))
         nc.sync.dma_start(w_codes[:], w_words[0].rearrange("p n t -> p (n t)").bitcast(I32))
-        for q in range(1, 4):
-            load_scales(q)
 
-        pairs = [keep.tile([P, 2, HALF, 2], BF16, name="pairs%d" % h, align_bytes=64) for h in range(2)]
+        pairs = [keep.tile([P, 2, HALF, 2], BF16, name="pairs%d" % h, tag="pairs%d" % h, align_bytes=512) for h in range(2)]
         cols = HALF // LIST_ROWS
         lists = [offsets[:, h * cols : (h + 1) * cols] for h in range(2)]
 
@@ -67,7 +66,7 @@ def tile_picked_pick_lin_bias_srt_e_kernel(tc, xT, w_words, w_scales, b, offs, o
                 window = planes[t][:, :SPLIT] if (t, h) == (PACK - 1, 0) else planes[t]
                 nc.vector.tensor_copy(pairs[h][:, t // 2, :, t % 2], window.indirect(lists[h]))
 
-        picked = [keep.tile([P, QUARTER * PACK], BF16, name="picked%d" % q, align_bytes=64) for q in range(4)]
+        picked = [keep.tile([P, QUARTER * PACK], BF16, name="picked%d" % q, tag="picked%d" % q, align_bytes=512) for q in range(4)]
         for q in range(4):
             h, u = divmod(q, 2)
             words = pairs[h][:].rearrange("p a n e -> p (a n e)").bitcast(U32).rearrange("p (a n) -> p n a", a=2)
@@ -85,11 +84,13 @@ def tile_picked_pick_lin_bias_srt_e_kernel(tc, xT, w_words, w_scales, b, offs, o
         for q in range(4):
             nc.vector.quantize_mx(out=x_codes[q][:].bitcast(FP8X4), scales=x_bytes[q][:], in_=picked[q][:])
 
+        by_scalar = keep.tile([P, 2, HALF], F32, name="by_scalar", tag="pairs1", align_bytes=512)
+        by_vector = keep.tile([P, 2, HALF], F32, name="by_vector", tag="picked3", align_bytes=512)
         for h in range(2):
-            for c in range(N // P):
-                result = keep.tile([P, HALF], F32, name="result%d%d" % (h, c), align_bytes=512)
-                for u in range(2):
-                    q = 2 * h + u
+            results = [(by_scalar if c == h else by_vector)[:, h, :] for c in range(N // P)]
+            for u in range(2):
+                q = 2 * h + u
+                for c in range(N // P):
                     nc.tensor.matmul_mx(
                         out=acc[q][c][:],
                         lhsT=w_codes[:, c * P : (c + 1) * P].bitcast(FP8X4),
@@ -99,9 +100,10 @@ def tile_picked_pick_lin_bias_srt_e_kernel(tc, xT, w_words, w_scales, b, offs, o
                         start=True,
                         stop=True,
                     )
-                    piece = result[:, u * QUARTER : (u + 1) * QUARTER]
-                    if c == 1:
+                    piece = results[c][:, u * QUARTER : (u + 1) * QUARTER]
+                    if c == h:
                         nc.scalar.activation(piece, acc[q][c][:], IDENTITY, bias=bias[:, c : c + 1])
                     else:
                         nc.vector.tensor_scalar(piece, acc[q][c][:], bias[:, c : c + 1], None, ADD)
-                nc.sync.dma_start(out[c * P : (c + 1) * P, h * HALF : (h + 1) * HALF], result[:])
+            for c in range(N // P):
+                nc.sync.dma_start(out[c * P : (c + 1) * P, h * HALF : (h + 1) * HALF], results[c])

@@ -22,7 +22,9 @@ PACK = 4
 HALF = S // 2
 QUARTER = S // 4
 LIST_ROWS = 16
-SPLIT = T - S + HALF
+CUT = 224
+REST = S - CUT
+SPLIT = T - S + CUT
 
 
 def tile_picked_pick_lin_bias_srt_e_kernel(tc, xT, w_words, w_scales, b, offs, out):
@@ -40,70 +42,90 @@ def tile_picked_pick_lin_bias_srt_e_kernel(tc, xT, w_words, w_scales, b, offs, o
         bias_rows = keep.tile([P, P], F32, name="bias_rows", align_bytes=64)
         bias = keep.tile([P, N // P], F32, name="bias", align_bytes=64)
 
-        def load_scales(q):
-            nc.sync.dma_start(w_bytes[32 * q : 32 * q + 4, :].bitcast(I32), w_scales[0, 4 * q : 4 * q + 4, :].bitcast(I32))
-
+        nc.vector.memset(bias_rows[:], 0.0)
         nc.vector.memset(w_bytes[:].bitcast(I32), 0)
         nc.sync.dma_start(low[:], x_rows.rearrange("p t c -> p (t c)")[:, : 2 * T])
         nc.sync.dma_start(offsets[:], offs)
-        for q in range(4):
-            load_scales(q)
+        nc.sync.dma_start(bias_rows[: N // P, :], b.rearrange("(c p) o -> c (p o)", p=P))
         nc.sync.dma_start(planes[2][:], x_rows[:, 2, :])
         nc.sync.dma_start(planes[3][:, :SPLIT], x_rows[:, 3, :SPLIT])
         nc.sync.dma_start(planes[3][:, SPLIT:], x_rows[:, 3, SPLIT:])
-
-        nc.vector.memset(bias_rows[:], 0.0)
-
-        nc.sync.dma_start(bias_rows[: N // P, :], b.rearrange("(c p) o -> c (p o)", p=P))
         nc.sync.dma_start(w_codes[:], w_words[0].rearrange("p n t -> p (n t)").bitcast(I32))
-
-        pairs = [keep.tile([P, 2, HALF, 2], BF16, name="pairs%d" % h, tag="pairs%d" % h, align_bytes=512) for h in range(2)]
-        cols = HALF // LIST_ROWS
-        lists = [offsets[:, h * cols : (h + 1) * cols] for h in range(2)]
-
-        for t in range(PACK):
-            for h in range(2):
-                window = planes[t][:, :SPLIT] if (t, h) == (PACK - 1, 0) else planes[t]
-                nc.vector.tensor_copy(pairs[h][:, t // 2, :, t % 2], window.indirect(lists[h]))
-
-        picked = [keep.tile([P, QUARTER * PACK], BF16, name="picked%d" % q, tag="picked%d" % q, align_bytes=512) for q in range(4)]
         for q in range(4):
-            h, u = divmod(q, 2)
-            words = pairs[h][:].rearrange("p a n e -> p (a n e)").bitcast(U32).rearrange("p (a n) -> p n a", a=2)
-            nc.scalar.copy(picked[q][:].bitcast(U32).rearrange("p (n a) -> p n a", a=2), words[:, u * QUARTER : (u + 1) * QUARTER, :])
+            nc.sync.dma_start(w_bytes[32 * q : 32 * q + 4, :].bitcast(I32), w_scales[0, 4 * q : 4 * q + 4, :].bitcast(I32))
 
         acc = [[psum.tile([P, QUARTER], F32, name="acc%d%d" % (q, c)) for c in range(N // P)] for q in range(4)]
-        held = keep.tile([P, P], F32, name="held", tag="held", align_bytes=64)
-        make_identity(nc, held[:, :P])
-        nc.tensor.transpose(acc[3][1][:], bias_rows[:], held[:, :P])
+        ident = keep.tile([P, P], F32, name="ident", align_bytes=64)
+        make_identity(nc, ident[:])
+        nc.tensor.transpose(acc[3][1][:], bias_rows[:], ident[:])
         nc.scalar.activation(bias[:], acc[3][1][:, : N // P], COPY)
 
-        codes = keep.tile([P, S], U32, name="codes", tag="held", align_bytes=64)
-        x_codes = [codes[:, q * QUARTER : (q + 1) * QUARTER] for q in range(4)]
+        def entries(a, e):
+            return offsets[:, a // LIST_ROWS : e // LIST_ROWS]
+
+        first = keep.tile([P, PACK * CUT], BF16, name="first", align_bytes=512)[:]
+        first_pairs = first.rearrange("p (a n e) -> p a n e", a=2, e=2)
+        second_high = keep.tile([P, 2 * REST], BF16, name="second_high", align_bytes=512)[:]
+        second_low = keep.tile([P, REST, 2], BF16, name="second_low", align_bytes=512)
+        picked = [keep.tile([P, QUARTER * PACK], BF16, name="picked%d" % q, tag="picked%d" % q, align_bytes=512) for q in range(4)]
+
+        def spot(a, e):
+            q = a // QUARTER
+            return picked[q][:, (a - q * QUARTER) * PACK : (e - q * QUARTER) * PACK]
+
+        late = [(CUT, HALF), (HALF, HALF + QUARTER), (HALF + QUARTER, S)]
+        for t in range(2):
+            nc.vector.tensor_copy(first_pairs[:, 0, :, t], planes[t][:, :SPLIT].indirect(entries(0, CUT)))
+            nc.vector.tensor_copy(second_low[:, :, t], planes[t].indirect(entries(CUT, S)))
+        low_words = second_low[:].rearrange("p n e -> p (n e)").bitcast(U32)
+        for a, e in late:
+            nc.scalar.copy(spot(a, e).bitcast(U32).rearrange("p (n a) -> p n a", a=2)[:, :, 0], low_words[:, a - CUT : e - CUT])
+        nc.vector.tensor_copy(first_pairs[:, 1, :, 0], planes[2][:, :SPLIT].indirect(entries(0, CUT)))
+        nc.vector.tensor_copy(second_high[:, :REST], planes[2].indirect(entries(CUT, S)))
+        nc.vector.tensor_copy(first_pairs[:, 1, :, 1], planes[3][:, :SPLIT].indirect(entries(0, CUT)))
+        for a, e in ((CUT, HALF + QUARTER), (HALF + QUARTER, S)):
+            nc.vector.tensor_copy(second_high[:, REST + a - CUT : REST + e - CUT], planes[3].indirect(entries(a, e)))
+
+        first_words = first.bitcast(U32).rearrange("p (a n) -> p n a", a=2)
+        for a, e in ((0, QUARTER // 2), (QUARTER // 2, QUARTER), (QUARTER, CUT)):
+            nc.scalar.copy(spot(a, e).bitcast(U32).rearrange("p (n a) -> p n a", a=2), first_words[:, a:e, :])
+
+        x_codes = [keep.tile([P, QUARTER], U32, name="x_codes%d" % q, align_bytes=64) for q in range(4)]
         x_bytes = [keep.tile([P, QUARTER], U8, name="x_bytes%d" % q, align_bytes=64) for q in range(4)]
-        for q in range(4):
+
+        def quantise(q):
             nc.vector.quantize_mx(out=x_codes[q][:].bitcast(FP8X4), scales=x_bytes[q][:], in_=picked[q][:])
 
-        by_scalar = keep.tile([P, 2, HALF], F32, name="by_scalar", tag="pairs1", align_bytes=512)
-        by_vector = keep.tile([P, 2, HALF], F32, name="by_vector", tag="picked3", align_bytes=512)
-        for h in range(2):
-            results = [(by_scalar if c == h else by_vector)[:, h, :] for c in range(N // P)]
-            for u in range(2):
-                q = 2 * h + u
-                for c in range(N // P):
-                    nc.tensor.matmul_mx(
-                        out=acc[q][c][:],
-                        lhsT=w_codes[:, c * P : (c + 1) * P].bitcast(FP8X4),
-                        lhsT_scale=w_bytes[:, c * P : (c + 1) * P],
-                        rhs=x_codes[q][:].bitcast(FP8X4),
-                        rhs_scale=x_bytes[q][:],
-                        start=True,
-                        stop=True,
-                    )
-                    piece = results[c][:, u * QUARTER : (u + 1) * QUARTER]
-                    if c == h:
-                        nc.scalar.activation(piece, acc[q][c][:], IDENTITY, bias=bias[:, c : c + 1])
-                    else:
-                        nc.vector.tensor_scalar(piece, acc[q][c][:], bias[:, c : c + 1], None, ADD)
+        def high_words(a, e):
+            dst = spot(a, e).rearrange("p (n k) -> p n k", k=PACK)[:, :, 2:]
+            src = second_high.rearrange("p (e n) -> p n e", e=2)[:, a - CUT : e - CUT, :]
+            return dst, src
+
+        nc.scalar.copy(*high_words(*late[0]))
+        nc.scalar.copy(*high_words(*late[2]))
+        for a, e in ((0, QUARTER // 2), (QUARTER // 2, QUARTER)):
+            nc.vector.quantize_mx(out=x_codes[0][:, a:e].bitcast(FP8X4), scales=x_bytes[0][:, a:e], in_=spot(a, e))
+        nc.vector.tensor_copy(*high_words(*late[1]))
+        for q in range(1, 4):
+            quantise(q)
+
+        by_scalar = keep.tile([P, 2, N // P, QUARTER], F32, name="by_scalar", align_bytes=512)
+        by_vector = keep.tile([P, 2, N // P, QUARTER], F32, name="by_vector", tag="picked3", align_bytes=512)
+        out_rows = out.rearrange("(c p) s -> p c s", p=P)
+        for q in range(4):
+            results = (by_vector if q % 2 else by_scalar)[:, q // 2]
             for c in range(N // P):
-                nc.sync.dma_start(out[c * P : (c + 1) * P, h * HALF : (h + 1) * HALF], results[c])
+                nc.tensor.matmul_mx(
+                    out=acc[q][c][:],
+                    lhsT=w_codes[:, c * P : (c + 1) * P].bitcast(FP8X4),
+                    lhsT_scale=w_bytes[:, c * P : (c + 1) * P],
+                    rhs=x_codes[q][:].bitcast(FP8X4),
+                    rhs_scale=x_bytes[q][:],
+                    start=True,
+                    stop=True,
+                )
+                if q == 1 or (q, c) == (3, 0):
+                    nc.vector.tensor_scalar(results[:, c, :], acc[q][c][:], bias[:, c : c + 1], None, ADD)
+                else:
+                    nc.scalar.activation(results[:, c, :], acc[q][c][:], IDENTITY, bias=bias[:, c : c + 1])
+            nc.sync.dma_start(out_rows[:, :, q * QUARTER : (q + 1) * QUARTER], results)

@@ -102,12 +102,15 @@ def tile_picked_pick_lin_bias_srt_e_kernel(tc, xT, w_words, w_scales, b, offs, o
             return dst, src
 
         nc.scalar.copy(*high_words(*late[0]))
-        nc.scalar.copy(*high_words(*late[2]))
+        for a, e in late[1:]:
+            nc.scalar.copy(*high_words(a, (a + e) // 2))
         for a, e in ((0, QUARTER // 2), (QUARTER // 2, QUARTER)):
             nc.vector.quantize_mx(out=x_codes[0][:, a:e].bitcast(FP8X4), scales=x_bytes[0][:, a:e], in_=spot(a, e))
-        nc.vector.tensor_copy(*high_words(*late[1]))
-        for q in range(1, 4):
+        for q in (1, 2):
+            a, e = late[q]
+            nc.vector.tensor_copy(*high_words((a + e) // 2, e))
             quantise(q)
+        quantise(3)
 
         by_scalar = keep.tile([P, 2, N // P, QUARTER], F32, name="by_scalar", align_bytes=512)
         by_vector = keep.tile([P, 2, N // P, QUARTER], F32, name="by_vector", tag="picked3", align_bytes=512)

@@ -1,7 +1,6 @@
 from contextlib import ExitStack
 
 import concourse.mybir as mybir
-from concourse.masks import make_identity
 
 K, T, S, N = 512, 2048, 512, 256
 FLOPS = 2 * K * S * N
@@ -14,7 +13,6 @@ U16 = mybir.dt.uint16
 U8 = mybir.dt.uint8
 FP8X4 = mybir.dt.float8_e4m3fn_x4
 IDENTITY = mybir.ActivationFunctionType.Identity
-COPY = mybir.ActivationFunctionType.Copy
 ADD = mybir.AluOpType.add
 
 P = 128
@@ -25,6 +23,7 @@ LIST_ROWS = 16
 CUT = 224
 REST = S - CUT
 SPLIT = T - S + CUT
+BLOCK = 32
 
 
 def tile_picked_pick_lin_bias_srt_e_kernel(tc, xT, w_words, w_scales, b, offs, out):
@@ -39,14 +38,16 @@ def tile_picked_pick_lin_bias_srt_e_kernel(tc, xT, w_words, w_scales, b, offs, o
         x_rows = xT.rearrange("(p t) c -> p t c", t=PACK)
         w_codes = keep.tile([P, N], I32, name="w_codes", align_bytes=512)
         w_bytes = keep.tile([P, N], U8, name="w_bytes", align_bytes=64)
-        bias_rows = keep.tile([P, P], F32, name="bias_rows", align_bytes=64)
-        bias = keep.tile([P, N // P], F32, name="bias", align_bytes=64)
+        bias_rows = keep.tile([P, BLOCK], F32, name="bias_rows", align_bytes=64)
+        bias = keep.tile([P, BLOCK], F32, name="bias", align_bytes=64)
 
         nc.vector.memset(bias_rows[:], 0.0)
         nc.vector.memset(w_bytes[:].bitcast(I32), 0)
         nc.sync.dma_start(low[:], x_rows.rearrange("p t c -> p (t c)")[:, : 2 * T])
         nc.sync.dma_start(offsets[:], offs)
-        nc.sync.dma_start(bias_rows[: N // P, :], b.rearrange("(c p) o -> c (p o)", p=P))
+        bias_runs = b.rearrange("(c q i) o -> c q (i o)", c=N // P, i=BLOCK)
+        for c in range(N // P):
+            nc.sync.dma_start(bias_rows[c:P:BLOCK, :], bias_runs[c])
         nc.sync.dma_start(planes[2][:], x_rows[:, 2, :])
         nc.sync.dma_start(planes[3][:, :SPLIT], x_rows[:, 3, :SPLIT])
         nc.sync.dma_start(planes[3][:, SPLIT:], x_rows[:, 3, SPLIT:])
@@ -55,10 +56,7 @@ def tile_picked_pick_lin_bias_srt_e_kernel(tc, xT, w_words, w_scales, b, offs, o
             nc.sync.dma_start(w_bytes[32 * q : 32 * q + 4, :].bitcast(I32), w_scales[0, 4 * q : 4 * q + 4, :].bitcast(I32))
 
         acc = [[psum.tile([P, QUARTER], F32, name="acc%d%d" % (q, c)) for c in range(N // P)] for q in range(4)]
-        ident = keep.tile([P, P], F32, name="ident", align_bytes=64)
-        make_identity(nc, ident[:])
-        nc.tensor.transpose(acc[3][1][:], bias_rows[:], ident[:])
-        nc.scalar.activation(bias[:], acc[3][1][:, : N // P], COPY)
+        nc.vector.transpose(bias[:], bias_rows[:])
 
         def entries(a, e):
             return offsets[:, a // LIST_ROWS : e // LIST_ROWS]

@@ -63,7 +63,7 @@ def tile_picked_pick_lin_bias_srt_e_kernel(tc, xT, w_words, w_scales, b, offs, o
 
         first = keep.tile([P, PACK * CUT], BF16, name="first", align_bytes=512)[:]
         first_pairs = first.rearrange("p (a n e) -> p a n e", a=2, e=2)
-        second_high = keep.tile([P, 2 * REST], BF16, name="second_high", align_bytes=512)[:]
+        second_high = [keep.tile([P, REST], BF16, name="second_high%d" % t, align_bytes=64) for t in (2, 3)]
         second_low = keep.tile([P, REST, 2], BF16, name="second_low", align_bytes=512)
         picked = [keep.tile([P, QUARTER * PACK], BF16, name="picked%d" % q, tag="picked%d" % q, align_bytes=512) for q in range(4)]
 
@@ -78,11 +78,18 @@ def tile_picked_pick_lin_bias_srt_e_kernel(tc, xT, w_words, w_scales, b, offs, o
         low_words = second_low[:].rearrange("p n e -> p (n e)").bitcast(U32)
         for a, e in late:
             nc.scalar.copy(spot(a, e).bitcast(U32).rearrange("p (n a) -> p n a", a=2)[:, :, 0], low_words[:, a - CUT : e - CUT])
+
+        def insert(copy, t, a, e):
+            source = second_high[t - 2]
+            copy(spot(a, e).rearrange("p (n k) -> p n k", k=PACK)[:, :, t], source[:, a - CUT : e - CUT])
+
+        nc.vector.tensor_copy(second_high[0][:], planes[2].indirect(entries(CUT, S)))
+        for a, e in late:
+            insert(nc.scalar.copy, 2, a, e)
         nc.vector.tensor_copy(first_pairs[:, 1, :, 0], planes[2][:, :SPLIT].indirect(entries(0, CUT)))
-        nc.vector.tensor_copy(second_high[:, :REST], planes[2].indirect(entries(CUT, S)))
         nc.vector.tensor_copy(first_pairs[:, 1, :, 1], planes[3][:, :SPLIT].indirect(entries(0, CUT)))
         for a, e in ((CUT, HALF + QUARTER), (HALF + QUARTER, S)):
-            nc.vector.tensor_copy(second_high[:, REST + a - CUT : REST + e - CUT], planes[3].indirect(entries(a, e)))
+            nc.vector.tensor_copy(second_high[1][:, a - CUT : e - CUT], planes[3].indirect(entries(a, e)))
 
         first_words = first.bitcast(U32).rearrange("p (a n) -> p n a", a=2)
         for a, e in ((0, QUARTER // 2), (QUARTER // 2, QUARTER), (QUARTER, CUT)):
@@ -94,19 +101,14 @@ def tile_picked_pick_lin_bias_srt_e_kernel(tc, xT, w_words, w_scales, b, offs, o
         def quantise(q):
             nc.vector.quantize_mx(out=x_codes[q][:].bitcast(FP8X4), scales=x_bytes[q][:], in_=picked[q][:])
 
-        def high_words(a, e):
-            dst = spot(a, e).rearrange("p (n k) -> p n k", k=PACK)[:, :, 2:]
-            src = second_high.rearrange("p (e n) -> p n e", e=2)[:, a - CUT : e - CUT, :]
-            return dst, src
-
-        nc.scalar.copy(*high_words(*late[0]))
+        insert(nc.scalar.copy, 3, *late[0])
         for a, e in late[1:]:
-            nc.scalar.copy(*high_words(a, (a + e) // 2))
+            insert(nc.scalar.copy, 3, a, (a + e) // 2)
         for a, e in ((0, QUARTER // 2), (QUARTER // 2, QUARTER)):
             nc.vector.quantize_mx(out=x_codes[0][:, a:e].bitcast(FP8X4), scales=x_bytes[0][:, a:e], in_=spot(a, e))
         for q in (1, 2):
             a, e = late[q]
-            nc.vector.tensor_copy(*high_words((a + e) // 2, e))
+            insert(nc.vector.tensor_copy, 3, (a + e) // 2, e)
             quantise(q)
         quantise(3)
 

from contextlib import ExitStack

import concourse.mybir as mybir

K, T, S, N = 512, 2048, 512, 256
FLOPS = 2 * K * S * N

F32 = mybir.dt.float32
BF16 = mybir.dt.bfloat16
I32 = mybir.dt.int32
U32 = mybir.dt.uint32
U16 = mybir.dt.uint16
U8 = mybir.dt.uint8
FP8X4 = mybir.dt.float8_e4m3fn_x4
IDENTITY = mybir.ActivationFunctionType.Identity
ADD = mybir.AluOpType.add

P = 128
PACK = 4
HALF = S // 2
QUARTER = S // 4
LIST_ROWS = 16
CUT = 224
REST = S - CUT
SPLIT = T - S + CUT
BLOCK = 32


def tile_picked_pick_lin_bias_srt_e_kernel(tc, xT, w_words, w_scales, b, offs, out):
    nc = tc.nc
    with ExitStack() as ctx:
        keep = ctx.enter_context(tc.tile_pool(name="keep", bufs=1))
        psum = ctx.enter_context(tc.psum_pool(name="psum", bufs=1))

        offsets = keep.tile([P, S // LIST_ROWS], U16, name="offsets")
        low = keep.tile([P, 2 * T], F32, name="low", align_bytes=512)
        planes = [low[:, :T], low[:, T:]] + [keep.tile([P, T], F32, name="plane%d" % t, align_bytes=512)[:] for t in (2, 3)]
        x_rows = xT.rearrange("(p t) c -> p t c", t=PACK)
        w_codes = keep.tile([P, N], I32, name="w_codes", align_bytes=512)
        w_bytes = keep.tile([P, N], U8, name="w_bytes", align_bytes=64)
        bias_rows = keep.tile([P, BLOCK], F32, name="bias_rows", align_bytes=64)
        bias = keep.tile([P, BLOCK], F32, name="bias", align_bytes=64)

        nc.vector.memset(bias_rows[:], 0.0)
        nc.vector.memset(w_bytes[:].bitcast(I32), 0)
        nc.sync.dma_start(low[:], x_rows.rearrange("p t c -> p (t c)")[:, : 2 * T])
        nc.sync.dma_start(offsets[:], offs)
        bias_runs = b.rearrange("(c q i) o -> c q (i o)", c=N // P, i=BLOCK)
        for c in range(N // P):
            nc.sync.dma_start(bias_rows[c:P:BLOCK, :], bias_runs[c])
        nc.sync.dma_start(planes[2][:], x_rows[:, 2, :])
        nc.sync.dma_start(planes[3][:, :SPLIT], x_rows[:, 3, :SPLIT])
        nc.sync.dma_start(planes[3][:, SPLIT:], x_rows[:, 3, SPLIT:])
        nc.sync.dma_start(w_codes[:], w_words[0].rearrange("p n t -> p (n t)").bitcast(I32))
        for q in range(4):
            nc.sync.dma_start(w_bytes[32 * q : 32 * q + 4, :].bitcast(I32), w_scales[0, 4 * q : 4 * q + 4, :].bitcast(I32))

        acc = [[psum.tile([P, QUARTER], F32, name="acc%d%d" % (q, c)) for c in range(N // P)] for q in range(4)]
        nc.vector.transpose(bias[:], bias_rows[:])

        def entries(a, e):
            return offsets[:, a // LIST_ROWS : e // LIST_ROWS]

        first = keep.tile([P, PACK * CUT], BF16, name="first", align_bytes=512)[:]
        first_pairs = first.rearrange("p (a n e) -> p a n e", a=2, e=2)
        second_high = [keep.tile([P, REST], BF16, name="second_high%d" % t, align_bytes=64) for t in (2, 3)]
        second_low = keep.tile([P, REST, 2], BF16, name="second_low", align_bytes=512)
        picked = [keep.tile([P, QUARTER * PACK], BF16, name="picked%d" % q, tag="picked%d" % q, align_bytes=512) for q in range(4)]

        def spot(a, e):
            q = a // QUARTER
            return picked[q][:, (a - q * QUARTER) * PACK : (e - q * QUARTER) * PACK]

        late = [(CUT, HALF), (HALF, HALF + QUARTER), (HALF + QUARTER, S)]
        for t in range(2):
            nc.vector.tensor_copy(first_pairs[:, 0, :, t], planes[t][:, :SPLIT].indirect(entries(0, CUT)))
            nc.vector.tensor_copy(second_low[:, :, t], planes[t].indirect(entries(CUT, S)))
        low_words = second_low[:].rearrange("p n e -> p (n e)").bitcast(U32)
        for a, e in late:
            nc.scalar.copy(spot(a, e).bitcast(U32).rearrange("p (n a) -> p n a", a=2)[:, :, 0], low_words[:, a - CUT : e - CUT])

        def insert(copy, t, a, e):
            source = second_high[t - 2]
            copy(spot(a, e).rearrange("p (n k) -> p n k", k=PACK)[:, :, t], source[:, a - CUT : e - CUT])

        nc.vector.tensor_copy(second_high[0][:], planes[2].indirect(entries(CUT, S)))
        for a, e in late:
            insert(nc.scalar.copy, 2, a, e)
        nc.vector.tensor_copy(first_pairs[:, 1, :, 0], planes[2][:, :SPLIT].indirect(entries(0, CUT)))
        nc.vector.tensor_copy(first_pairs[:, 1, :, 1], planes[3][:, :SPLIT].indirect(entries(0, CUT)))
        for a, e in ((CUT, HALF + QUARTER), (HALF + QUARTER, S)):
            nc.vector.tensor_copy(second_high[1][:, a - CUT : e - CUT], planes[3].indirect(entries(a, e)))

        first_words = first.bitcast(U32).rearrange("p (a n) -> p n a", a=2)
        for a, e in ((0, QUARTER // 2), (QUARTER // 2, QUARTER), (QUARTER, CUT)):
            nc.scalar.copy(spot(a, e).bitcast(U32).rearrange("p (n a) -> p n a", a=2), first_words[:, a:e, :])

        x_codes = [keep.tile([P, QUARTER], U32, name="x_codes%d" % q, align_bytes=64) for q in range(4)]
        x_bytes = [keep.tile([P, QUARTER], U8, name="x_bytes%d" % q, align_bytes=64) for q in range(4)]

        def quantise(q):
            nc.vector.quantize_mx(out=x_codes[q][:].bitcast(FP8X4), scales=x_bytes[q][:], in_=picked[q][:])

        insert(nc.scalar.copy, 3, *late[0])
        for a, e in late[1:]:
            insert(nc.scalar.copy, 3, a, (a + e) // 2)
        for a, e in ((0, QUARTER // 2), (QUARTER // 2, QUARTER)):
            nc.vector.quantize_mx(out=x_codes[0][:, a:e].bitcast(FP8X4), scales=x_bytes[0][:, a:e], in_=spot(a, e))
        for q in (1, 2):
            a, e = late[q]
            insert(nc.vector.tensor_copy, 3, (a + e) // 2, e)
            quantise(q)
        quantise(3)

        by_scalar = keep.tile([P, 2, N // P, QUARTER], F32, name="by_scalar", align_bytes=512)
        by_vector = keep.tile([P, 2, N // P, QUARTER], F32, name="by_vector", tag="picked3", align_bytes=512)
        out_rows = out.rearrange("(c p) s -> p c s", p=P)
        for q in range(4):
            results = (by_vector if q % 2 else by_scalar)[:, q // 2]
            for c in range(N // P):
                nc.tensor.matmul_mx(
                    out=acc[q][c][:],
                    lhsT=w_codes[:, c * P : (c + 1) * P].bitcast(FP8X4),
                    lhsT_scale=w_bytes[:, c * P : (c + 1) * P],
                    rhs=x_codes[q][:].bitcast(FP8X4),
                    rhs_scale=x_bytes[q][:],
                    start=True,
                    stop=True,
                )
                if q == 1 or (q, c) == (3, 0):
                    nc.vector.tensor_scalar(results[:, c, :], acc[q][c][:], bias[:, c : c + 1], None, ADD)
                else:
                    nc.scalar.activation(results[:, c, :], acc[q][c][:], IDENTITY, bias=bias[:, c : c + 1])
            nc.sync.dma_start(out_rows[:, :, q * QUARTER : (q + 1) * QUARTER], results)
